import numpy as np
CORES = [127,119,111,103,95,87,79,71,63,55,47,39,31,23,15,7]
N = 16
H = 2
PERIODIC = True
def setup_inputs(rng):
    return {"x": rng.standard_normal((N, 128, 256), dtype=np.float32)}
def reference(x):
    W = x.shape[2]
    y = np.zeros((N, 128, W + 2 * H), x.dtype)
    for r in range(N):
        y[r][:, H:H + W] = x[r]
        left, right = r - 1, r + 1
        if PERIODIC:
            left, right = left % N, right % N
        if 0 <= left < N:
            y[r][:, :H] = x[left][:, W - H:]
        if 0 <= right < N:
            y[r][:, W + H:] = x[right][:, :H]
    return {"y": y}

@@ -1,0 +1,44 @@
+from concourse.bass import DstId, RemoteDMATransfer
+
+H = 2
+
+SCRATCH = {
+    "send": ("dram", [2, 128, H], "float32"),
+    "recv": ("dram", [2, 128, H], "float32"),
+}
+SEMAPHORES = ["loaded", "sent", "arr_l", "arr_r", "done"]
+
+
+def rank_program(g, core, T, topo):
+    rank = T.rank_of(core)
+    if rank is None:
+        return
+    n = len(T.cores)
+    W = T.x.shape[1]
+    left = T.cores[(rank - 1) % n]
+    right = T.cores[(rank + 1) % n]
+    s = T.sem
+    q_l, q_r = g.sync, g.scalar
+
+    q_l.dma_start(T.send[0], T.x[:, 0:H]).then_inc(s.loaded, 16)
+    q_r.dma_start(T.send[1], T.x[:, W - H:W]).then_inc(s.loaded, 16)
+
+    def transfer(dst_core, src, dst, sem, engine):
+        rid, pid, _se = topo.addr(dst_core)
+        return RemoteDMATransfer(dst_ids=[DstId(rid=rid, pnc=pid)], dma_engine_mask=1 << engine,
+                                 remote_sem=sem, src=src, dst=dst)
+
+    g.wait_ge(s.loaded, 32)
+    g.remote_dma_fused([transfer(left, T.send[0], T.recv[1], s.arr_r, 0),
+                        transfer(right, T.send[1], T.recv[0], s.arr_l, 1)], local_sem=s.sent)
+
+    q_far = q_r if topo.mates(topo.chip(core), topo.chip(left)) else q_l
+    q_far.wait_ge(s.sent, 2)
+    q_far.dma_start(T.y[:, H:H + W], T.x[:]).then_inc(s.done, 16)
+
+    q_l.wait_ge(s.arr_l, 1)
+    q_l.dma_start(T.y[:, 0:H], T.recv[0]).then_inc(s.done, 16)
+    q_r.wait_ge(s.arr_r, 1)
+    q_r.dma_start(T.y[:, H + W:H + W + H], T.recv[1]).then_inc(s.done, 16)
+
+    g.wait_ge(s.done, 48)

@@ -1,12 +1,10 @@
-from concourse.bass import DstId, RemoteDMATransfer
-
 H = 2
 
 SCRATCH = {
     "send": ("dram", [2, 128, H], "float32"),
     "recv": ("dram", [2, 128, H], "float32"),
 }
-SEMAPHORES = ["loaded", "sent", "arr_l", "arr_r", "done"]
+SEMAPHORES = ["ld_far", "ld_near", "sent", "arr_l", "arr_r", "done"]
 
 
 def rank_program(g, core, T, topo):
@@ -15,30 +13,33 @@ def rank_program(g, core, T, topo):
         return
     n = len(T.cores)
     W = T.x.shape[1]
-    left = T.cores[(rank - 1) % n]
-    right = T.cores[(rank + 1) % n]
     s = T.sem
-    q_l, q_r = g.sync, g.scalar
+    nb = [T.cores[(rank - 1) % n], T.cores[(rank + 1) % n]]
+    edge = [T.x[:, 0:H], T.x[:, W - H:W]]
+    halo = [T.y[:, 0:H], T.y[:, H + W:H + W + H]]
+    arr = [s.arr_l, s.arr_r]
+    near = 0 if topo.mates(topo.chip(core), topo.chip(nb[0])) else 1
+    far = 1 - near
+    q = [None, None]
+    q[far], q[near] = g.sync, g.scalar
 
-    q_l.dma_start(T.send[0], T.x[:, 0:H]).then_inc(s.loaded, 16)
-    q_r.dma_start(T.send[1], T.x[:, W - H:W]).then_inc(s.loaded, 16)
+    q[far].dma_start(T.send[far], edge[far]).then_inc(s.ld_far, 16)
+    q[near].dma_start(T.send[near], edge[near]).then_inc(s.ld_near, 16)
 
-    def transfer(dst_core, src, dst, sem, engine):
-        rid, pid, _se = topo.addr(dst_core)
-        return RemoteDMATransfer(dst_ids=[DstId(rid=rid, pnc=pid)], dma_engine_mask=1 << engine,
-                                 remote_sem=sem, src=src, dst=dst)
+    def send(side, engine):
+        rid, pid, _se = topo.addr(nb[side])
+        g.remote_dma(T.recv[1 - side], T.send[side], arr[1 - side], s.sent, pid, rid, 1 << engine)
 
-    g.wait_ge(s.loaded, 32)
-    g.remote_dma_fused([transfer(left, T.send[0], T.recv[1], s.arr_r, 0),
-                        transfer(right, T.send[1], T.recv[0], s.arr_l, 1)], local_sem=s.sent)
+    g.wait_ge(s.ld_far, 16)
+    send(far, 0)
+    g.wait_ge(s.ld_near, 16)
+    send(near, 1)
 
-    q_far = q_r if topo.mates(topo.chip(core), topo.chip(left)) else q_l
-    q_far.wait_ge(s.sent, 2)
-    q_far.dma_start(T.y[:, H:H + W], T.x[:]).then_inc(s.done, 16)
+    q[near].wait_ge(s.sent, 2)
+    q[near].dma_start(T.y[:, H:H + W], T.x[:]).then_inc(s.done, 16)
 
-    q_l.wait_ge(s.arr_l, 1)
-    q_l.dma_start(T.y[:, 0:H], T.recv[0]).then_inc(s.done, 16)
-    q_r.wait_ge(s.arr_r, 1)
-    q_r.dma_start(T.y[:, H + W:H + W + H], T.recv[1]).then_inc(s.done, 16)
+    for side in (near, far):
+        q[side].wait_ge(arr[side], 1)
+        q[side].dma_start(halo[side], T.recv[side]).then_inc(s.done, 16)
 
     g.wait_ge(s.done, 48)

@@ -1,4 +1,5 @@
 H = 2
+E = 2
 
 SCRATCH = {
     "send": ("dram", [2, 128, H], "float32"),
@@ -25,21 +26,21 @@ def rank_program(g, core, T, topo):
 
     q[far].dma_start(T.send[far], edge[far]).then_inc(s.ld_far, 16)
     q[near].dma_start(T.send[near], edge[near]).then_inc(s.ld_near, 16)
+    q[near].dma_start(T.y[:, H:H + W], T.x[:]).then_inc(s.done, 16)
 
-    def send(side, engine):
+    def send(side, first_engine):
         rid, pid, _se = topo.addr(nb[side])
-        g.remote_dma(T.recv[1 - side], T.send[side], arr[1 - side], s.sent, pid, rid, 1 << engine)
+        mask = ((1 << E) - 1) << first_engine
+        g.remote_dma(T.recv[1 - side], T.send[side], arr[1 - side], s.sent, pid, rid, mask)
 
     g.wait_ge(s.ld_far, 16)
     send(far, 0)
     g.wait_ge(s.ld_near, 16)
-    send(near, 1)
-
-    q[near].wait_ge(s.sent, 2)
-    q[near].dma_start(T.y[:, H:H + W], T.x[:]).then_inc(s.done, 16)
+    send(near, E)
 
     for side in (near, far):
-        q[side].wait_ge(arr[side], 1)
+        q[side].wait_ge(arr[side], E)
         q[side].dma_start(halo[side], T.recv[side]).then_inc(s.done, 16)
 
+    g.wait_ge(s.sent, 2 * E)
     g.wait_ge(s.done, 48)

H = 2
E = 2

SCRATCH = {
    "send": ("dram", [2, 128, H], "float32"),
    "recv": ("dram", [2, 128, H], "float32"),
}
SEMAPHORES = ["ld_far", "ld_near", "sent", "arr_l", "arr_r", "done"]


def rank_program(g, core, T, topo):
    rank = T.rank_of(core)
    if rank is None:
        return
    n = len(T.cores)
    W = T.x.shape[1]
    s = T.sem
    nb = [T.cores[(rank - 1) % n], T.cores[(rank + 1) % n]]
    edge = [T.x[:, 0:H], T.x[:, W - H:W]]
    halo = [T.y[:, 0:H], T.y[:, H + W:H + W + H]]
    arr = [s.arr_l, s.arr_r]
    near = 0 if topo.mates(topo.chip(core), topo.chip(nb[0])) else 1
    far = 1 - near
    q = [None, None]
    q[far], q[near] = g.sync, g.scalar

    q[far].dma_start(T.send[far], edge[far]).then_inc(s.ld_far, 16)
    q[near].dma_start(T.send[near], edge[near]).then_inc(s.ld_near, 16)
    q[near].dma_start(T.y[:, H:H + W], T.x[:]).then_inc(s.done, 16)

    def send(side, first_engine):
        rid, pid, _se = topo.addr(nb[side])
        mask = ((1 << E) - 1) << first_engine
        g.remote_dma(T.recv[1 - side], T.send[side], arr[1 - side], s.sent, pid, rid, mask)

    g.wait_ge(s.ld_far, 16)
    send(far, 0)
    g.wait_ge(s.ld_near, 16)
    send(near, E)

    for side in (near, far):
        q[side].wait_ge(arr[side], E)
        q[side].dma_start(halo[side], T.recv[side]).then_inc(s.done, 16)

    g.wait_ge(s.sent, 2 * E)
    g.wait_ge(s.done, 48)
